import numpy as np
import ml_dtypes


def mxq(x, axis, fmt="e4m3"):
    dtype, down = {"e4m3": (ml_dtypes.float8_e4m3fn, 7), "e5m2": (ml_dtypes.float8_e5m2, 14)}[fmt]
    v = np.moveaxis(np.asarray(x, np.float32).astype(ml_dtypes.bfloat16).astype(np.float64), axis, -1)
    blocks = v.reshape(v.shape[:-1] + (-1, 32))
    amax = np.abs(blocks).max(-1, keepdims=True)
    byte = np.maximum(np.where(amax > 0, np.frexp(amax)[1] - 1 + 127, 0) - down, 1)
    scale = np.exp2(byte - 127.0)
    codes = (blocks / scale).astype(np.float32).astype(dtype).astype(np.float64)
    return np.moveaxis((codes * scale).reshape(v.shape), -1, axis)


WIDE = False


def mx_kscale(k):
    if not WIDE:
        return np.ones(k)
    levels = np.array([10, -10, 5, -5, 0])
    if k % 512:
        return np.exp2(np.random.permutation(np.resize(levels, k // 32))).repeat(32)
    a = np.empty((k // 512, 16))
    for p in range(k // 512):
        a[p, :8] = np.random.permutation(np.resize(levels, 8))
        for g in range(8):
            far = levels[np.abs(levels - a[p, g]) >= 10]
            a[p, g + 8] = far[np.random.randint(len(far))]
    return np.exp2(a.ravel()).repeat(32)


def f64(x):
    return np.asarray(x).astype(np.float64)


def striped8(idx):
    return np.asarray(idx).reshape(8, -1, 16).transpose(0, 2, 1).reshape(128, -1).astype(np.uint16)


def unstriped8(offs):
    return offs.reshape(8, 16, -1).transpose(0, 2, 1).reshape(8, -1).astype(np.int64)


def pick8(x, idx, run):
    r = np.arange(len(x))
    return x[r[:, None], idx[r % (8 * run) // run]]


E2M1 = np.array([0.0, 0.5, 1.0, 1.5, 2.0, 3.0, 4.0, 6.0, -0.0, -0.5, -1.0, -1.5, -2.0, -3.0, -4.0, -6.0])


def pack_weight(w, fmt):
    k, n = w.shape
    w = f64(np.asarray(w, np.float32).astype(ml_dtypes.bfloat16)).reshape(k // 32, 32, n)
    amax = np.abs(w).max(1)
    if fmt == "e4m3":
        byte = np.frexp(amax)[1] - 1 + 127 - 7
    else:
        mant, ex = np.frexp(amax / 6.0)
        byte = np.where(mant > 0.5, ex, ex - 1) + 127
    byte = np.clip(np.where(amax > 0, byte, 1), 1, 254)
    scaled = (w * np.exp2(127.0 - byte)[:, None, :]).reshape(k, n).astype(np.float32)
    by_word = np.ascontiguousarray(scaled.reshape(k // 512, 128, 4, n).transpose(0, 1, 3, 2))
    if fmt == "e4m3":
        words = by_word.astype(ml_dtypes.float8_e4m3fn).view(np.uint8)
    else:
        c = by_word.astype(ml_dtypes.float4_e2m1fn).view(np.uint8) & 0xF
        words = (c[..., 0::2] | (c[..., 1::2] << 4)).reshape(k // 512, 128, 2 * n)
    return np.ascontiguousarray(words), np.ascontiguousarray(byte.astype(np.uint8).reshape(k // 512, 16, n))


def unpack_weight(words, scales, fmt):
    g, _, n = scales.shape
    words = np.ascontiguousarray(words).reshape(g, 128, n, -1)
    if fmt == "e4m3":
        vals = words.view(ml_dtypes.float8_e4m3fn).astype(np.float64)
    else:
        nib = np.empty((g, 128, n, 4), np.uint8)
        nib[..., 0::2] = words & 0xF
        nib[..., 1::2] = words >> 4
        vals = E2M1[nib]
    vals = vals * np.repeat(np.exp2(scales.astype(np.float64) - 127.0), 8, axis=1)[..., None]
    return vals.transpose(0, 1, 3, 2).reshape(g * 512, n)


D, E, T, Q, I = 512, 512, 1024, 128, 512


def setup_inputs():
    n = np.random.standard_normal
    idx = np.stack([np.random.permutation(T)[:I] for _ in range(8)])
    idx2 = np.stack([np.random.permutation(T)[:I] for _ in range(8)])
    fd = mx_kscale(D)
    fe = mx_kscale(E)
    keysp = pack_weight(n((D, T)) / fd[:, None], "e2m1")
    return {
        "query": (n((D, Q)) * 0.7 / np.sqrt(D) * fd[:, None]).astype(np.float32),
        "keys_words": keysp[0],
        "keys_scales": keysp[1],
        "gout": (n((E, Q)) * 1 / np.sqrt(E) * fe[:, None]).astype(np.float32),
        "vals": (n((E, T)) / fe[:, None]).astype(np.float32),
        "old": (0.5 * n((Q, T))).astype(np.float32),
        "offs": striped8(idx),
        "offs2": striped8(idx2),
    }


def reference(query, keys_words, keys_scales, gout, vals, old, offs, offs2):
    idx = unstriped8(offs)
    idx2 = unstriped8(offs2)
    keysu = unpack_weight(keys_words, keys_scales, "e2m1")
    queryq = mxq(f64(query), 0, "e4m3")
    a = queryq.T @ keysu
    s = pick8(a, idx, 16) * pick8(a, idx2, 16) + (pick8(a, idx, 16) + pick8(a, idx2, 16)) * 0.5
    p = np.exp(s - np.max(s, axis=1, keepdims=True))
    z = np.sum(p, axis=1, keepdims=True)
    goutq = mxq(f64(gout), 0, "e4m3")
    valsq = mxq(f64(vals), 0, "e4m3")
    c0 = goutq.T @ valsq
    dw = pick8(c0, idx, 16)
    dz = np.sum(dw * p / np.square(z) * (-1.0), axis=1, keepdims=True)
    dp = dw / z + dz
    ds = dp * p
    e1 = ds * pick8(a, idx2, 16)
    s1 = np.zeros((Q, T))
    s1[np.arange(Q)[:, None], idx[np.arange(Q) % 128 // 16]] = e1
    e2 = ds * 0.5
    s2 = np.zeros((Q, T))
    s2[np.arange(Q)[:, None], idx[np.arange(Q) % 128 // 16]] = e2
    e3 = ds * pick8(a, idx, 16)
    s3 = np.zeros((Q, T))
    s3[np.arange(Q)[:, None], idx2[np.arange(Q) % 128 // 16]] = e3
    e4 = ds * 0.5
    s4 = np.zeros((Q, T))
    s4[np.arange(Q)[:, None], idx2[np.arange(Q) % 128 // 16]] = e4
    da = s1 + s2 + s3 + s4
    y = da * 512.0 + f64(old)
    return y

from contextlib import ExitStack

import concourse.mybir as mybir
from concourse.masks import make_identity

D, E, T, Q, I = 512, 512, 1024, 128, 512
FLOPS = 2 * D * Q * T + 2 * E * Q * T

F32 = mybir.dt.float32
BF16 = mybir.dt.bfloat16
I32 = mybir.dt.int32
U32 = mybir.dt.uint32
U16 = mybir.dt.uint16
U8 = mybir.dt.uint8
FP8X4 = mybir.dt.float8_e4m3fn_x4
FP4X4 = mybir.dt.float4_e2m1fn_x4
ALU = mybir.AluOpType
ACT = mybir.ActivationFunctionType
AXIS = mybir.AxisListType

P = 128
PACK = 4
BANK = 512
CHUNK = 256
N_CHUNKS = T // CHUNK
LAST_ON_VECTOR = 160


def interleave(copy, grouped, raw, c0, c1):
    copy(
        grouped[:, PACK * c0 : PACK * c1].rearrange("p (c i j) -> p c j i", i=4, j=PACK),
        raw[:, :, c0:c1].rearrange("p j (c i) -> p c j i", i=4),
    )


def tile_attend_bproductpairs_heads_kernel(tc, query, keys_words, keys_scales, gout, vals, old, offs, offs2, out):
    nc = tc.nc
    with ExitStack() as ctx:
        sb = ctx.enter_context(tc.tile_pool(name="sb", bufs=1))
        ps = ctx.enter_context(tc.psum_pool(name="ps", bufs=1))

        list1 = sb.tile([P, I // 16], U16, name="list1")
        list2 = sb.tile([P, I // 16], U16, name="list2")

        q_raw = sb.tile([P, PACK, Q], F32, name="q_raw")
        nc.sync.dma_start(out=q_raw[:], in_=query.rearrange("(p j) q -> p j q", j=PACK))
        k_scales = sb.tile([P, T], U8, name="k_scales", align_bytes=64)
        for quad in range(4):
            nc.sync.dma_start(
                out=k_scales[32 * quad : 32 * quad + 4, :].bitcast(I32),
                in_=keys_scales[0][4 * quad : 4 * quad + 4, :].bitcast(I32),
            )
        k_words = sb.tile([P, 2 * T], U8, name="k_words", align_bytes=64)
        nc.sync.dma_start(out=k_words[:].bitcast(I32), in_=keys_words[0].bitcast(I32))
        g_raw = sb.tile([P, PACK, Q], F32, name="g_raw")
        nc.sync.dma_start(out=g_raw[:], in_=gout.rearrange("(p j) q -> p j q", j=PACK))
        v_view = vals.rearrange("(p j) t -> p j t", j=PACK)
        v_raw = [sb.tile([P, PACK, CHUNK], F32, name="v_raw%d" % c, tag="v_raw%d" % c) for c in range(N_CHUNKS)]
        nc.sync.dma_start(out=v_raw[0][:], in_=v_view[:, :, 0:CHUNK])
        nc.sync.dma_start(list1[:], offs)
        nc.sync.dma_start(list2[:], offs2)
        for c in range(1, N_CHUNKS):
            nc.sync.dma_start(out=v_raw[c][:], in_=v_view[:, :, c * CHUNK : (c + 1) * CHUNK])
        old_sb = sb.tile([P, T], F32, name="old_sb")
        nc.sync.dma_start(out=old_sb[:], in_=old)

        warm_in = sb.tile([P, 1], F32, name="warm_in")
        warm_out = sb.tile([P, 1], F32, name="warm_out")
        nc.vector.memset(warm_in[:], 0.0)
        nc.scalar.activation(warm_out[:], warm_in[:], ACT.Exp)

        placed1 = sb.tile([P, T], F32, name="placed1")
        placed2 = sb.tile([P, T], F32, name="placed2")
        nc.vector.memset(placed1[:], 0.0)
        nc.vector.memset(placed2[:], 0.0)
        ident = sb.tile([P, P], F32, name="ident")
        make_identity(nc, ident[:])

        q_bf = sb.tile([P, PACK * Q], BF16, name="q_bf", align_bytes=64)
        q_codes = sb.tile([P, Q], U32, name="q_codes", align_bytes=64)
        q_scales = sb.tile([P, Q], U8, name="q_scales", align_bytes=64)
        interleave(nc.vector.tensor_copy, q_bf, q_raw, 0, Q)
        nc.vector.quantize_mx(out=q_codes[:].bitcast(FP8X4), scales=q_scales[:], in_=q_bf[:])

        a_sb = sb.tile([P, T], F32, name="a_sb")
        a_ps = [ps.tile([P, CHUNK], F32, name="a_ps%d" % c, tag="bank%d" % c) for c in range(N_CHUNKS)]
        for c in range(N_CHUNKS):
            nc.tensor.matmul_mx(
                out=a_ps[c][:],
                lhsT=q_codes[:].bitcast(FP8X4),
                lhsT_scale=q_scales[:],
                rhs=k_words[:, 2 * CHUNK * c : 2 * CHUNK * (c + 1)].bitcast(FP4X4),
                rhs_scale=k_scales[:, CHUNK * c : CHUNK * (c + 1)],
                start=True,
                stop=True,
            )
        g_bf = sb.tile([P, PACK * Q], BF16, name="g_bf", align_bytes=64)
        g_codes = sb.tile([P, Q], U32, name="g_codes", align_bytes=64)
        g_scales = sb.tile([P, Q], U8, name="g_scales", align_bytes=64)
        interleave(nc.scalar.copy, g_bf, g_raw, 0, Q)
        nc.vector.quantize_mx(out=g_codes[:].bitcast(FP8X4), scales=g_scales[:], in_=g_bf[:])
        for c in range(N_CHUNKS):
            copy = nc.vector.tensor_copy if c % 2 == 0 else nc.scalar.copy
            copy(a_sb[:, c * CHUNK : (c + 1) * CHUNK], a_ps[c][:])

        u1 = sb.tile([P, I], F32, name="u1")
        u2 = sb.tile([P, I], F32, name="u2")
        nc.vector.tensor_scalar(u1[:], a_sb[:].indirect(list1[:]), 1.0, 0.5, ALU.mult, ALU.add)
        nc.vector.tensor_scalar(u2[:], a_sb[:].indirect(list2[:]), 1.0, 0.5, ALU.mult, ALU.add)

        v_bf = [sb.tile([P, PACK * CHUNK], BF16, name="v_bf%d" % c, tag="v_bf%d" % c, align_bytes=64) for c in range(N_CHUNKS)]
        v_codes = [sb.tile([P, CHUNK], U32, name="v_codes%d" % c, align_bytes=64) for c in range(N_CHUNKS)]
        v_scales = [sb.tile([P, CHUNK], U8, name="v_scales%d" % c, align_bytes=64) for c in range(N_CHUNKS)]
        c_ps = [ps.tile([P, CHUNK], F32, name="c_ps%d" % c) for c in range(N_CHUNKS)]
        last = N_CHUNKS - 1

        def quantise_and_multiply(c):
            nc.vector.quantize_mx(out=v_codes[c][:].bitcast(FP8X4), scales=v_scales[c][:], in_=v_bf[c][:])
            nc.tensor.matmul_mx(
                out=c_ps[c][:],
                lhsT=g_codes[:].bitcast(FP8X4),
                lhsT_scale=g_scales[:],
                rhs=v_codes[c][:].bitcast(FP8X4),
                rhs_scale=v_scales[c][:],
                start=True,
                stop=True,
            )

        for c in range(N_CHUNKS - 1):
            interleave(nc.scalar.copy, v_bf[c], v_raw[c], 0, CHUNK)

        for c in range(last - 1):
            quantise_and_multiply(c)
        interleave(nc.vector.tensor_copy, v_bf[last], v_raw[last], 0, LAST_ON_VECTOR)
        interleave(nc.scalar.copy, v_bf[last], v_raw[last], LAST_ON_VECTOR, CHUNK)
        quantise_and_multiply(last - 1)
        s = sb.tile([P, I], F32, name="s", tag="v_bf%d" % (last - 1), align_bytes=64)
        nc.vector.tensor_tensor(s[:], u1[:], u2[:], ALU.mult)
        quantise_and_multiply(last)
        neg_max = sb.tile([P, 1], F32, name="neg_max", tag="v_bf%d" % last, align_bytes=64)
        nc.vector.tensor_reduce(neg_max[:], s[:], AXIS.X, ALU.max, negate=True)
        c_sb = sb.tile([P, T], F32, name="c_sb", tag="v_raw%d" % last)
        for c in range(N_CHUNKS):
            nc.scalar.copy(c_sb[:, c * CHUNK : (c + 1) * CHUNK], c_ps[c][:])
        p = sb.tile([P, I], F32, name="p")
        z = sb.tile([P, 1], F32, name="z")
        nc.scalar.activation(p[:], s[:], ACT.Exp, bias=neg_max[:], accum_out=z[:])

        dw = sb.tile([P, I], F32, name="dw")
        nc.vector.tensor_scalar(dw[:], c_sb[:].indirect(list1[:]), 512.0, 0.0, ALU.mult, ALU.add)
        inv_z = sb.tile([P, 1], F32, name="inv_z")
        nc.vector.reciprocal(inv_z[:], z[:])
        w = sb.tile([P, I], F32, name="w")
        nc.scalar.activation(w[:], p[:], ACT.Copy, scale=inv_z[:])
        weighted = sb.tile([P, I], F32, name="weighted")
        mean = sb.tile([P, 1], F32, name="mean")
        nc.vector.scalar_tensor_tensor(weighted[:], dw[:], inv_z[:], p[:], ALU.mult, ALU.mult, accum_out=mean[:])
        ds = sb.tile([P, I], F32, name="ds")
        nc.vector.scalar_tensor_tensor(ds[:], dw[:], mean[:], w[:], ALU.subtract, ALU.mult)

        nc.vector.tensor_tensor(placed1[:].indirect(list1[:]), ds[:], u2[:], ALU.mult)
        nc.vector.tensor_tensor(placed2[:].indirect(list2[:]), ds[:], u1[:], ALU.mult)

        turned_ps = [ps.tile([P, BANK], F32, name="turned_ps%d" % h, tag="bank%d" % h) for h in range(2)]
        turned_sb = [sb.tile([P, BANK], F32, name="turned_sb%d" % h) for h in range(2)]
        part_ps = [ps.tile([P, BANK], F32, name="part_ps%d" % h, tag="bank%d" % (2 + h)) for h in range(2)]
        blocks = BANK // P
        for source, first, final in ((old_sb, True, False), (placed1, False, True)):
            for h in range(2):
                for b in range(blocks):
                    nc.tensor.matmul(
                        turned_ps[h][:, b * P : (b + 1) * P],
                        source[:, h * BANK + b * P : h * BANK + (b + 1) * P],
                        ident[:],
                        start=(first and b == 0),
                        stop=(final and b == blocks - 1),
                        is_transpose=True,
                    )
        result = [sb.tile([P, BANK], F32, name="result%d" % h) for h in range(2)]
        for h in range(2):
            nc.scalar.copy(turned_sb[h][:], turned_ps[h][:])
            for b in range(blocks):
                nc.tensor.transpose(part_ps[h][:, b * P : (b + 1) * P], turned_sb[h][:, b * P : (b + 1) * P], ident[:])
        for h in range(2):
            nc.vector.tensor_tensor(result[h][:], part_ps[h][:], placed2[:, h * BANK : (h + 1) * BANK], ALU.add)
            nc.sync.dma_start(out=out[:, h * BANK : (h + 1) * BANK], in_=result[h][:])
